import numpy as np
import ml_dtypes


def mxq(x, axis, fmt="e4m3"):
    dtype, down = {"e4m3": (ml_dtypes.float8_e4m3fn, 7), "e5m2": (ml_dtypes.float8_e5m2, 14)}[fmt]
    v = np.moveaxis(np.asarray(x, np.float32).astype(ml_dtypes.bfloat16).astype(np.float64), axis, -1)
    blocks = v.reshape(v.shape[:-1] + (-1, 32))
    amax = np.abs(blocks).max(-1, keepdims=True)
    byte = np.maximum(np.where(amax > 0, np.frexp(amax)[1] - 1 + 127, 0) - down, 1)
    scale = np.exp2(byte - 127.0)
    codes = (blocks / scale).astype(np.float32).astype(dtype).astype(np.float64)
    return np.moveaxis((codes * scale).reshape(v.shape), -1, axis)


WIDE = False


def mx_kscale(k):
    if not WIDE:
        return np.ones(k)
    levels = np.array([10, -10, 5, -5, 0])
    if k % 512:
        return np.exp2(np.random.permutation(np.resize(levels, k // 32))).repeat(32)
    a = np.empty((k // 512, 16))
    for p in range(k // 512):
        a[p, :8] = np.random.permutation(np.resize(levels, 8))
        for g in range(8):
            far = levels[np.abs(levels - a[p, g]) >= 10]
            a[p, g + 8] = far[np.random.randint(len(far))]
    return np.exp2(a.ravel()).repeat(32)


def f64(x):
    return np.asarray(x).astype(np.float64)


def striped(idx):
    return np.tile(idx.reshape(-1, 16).T, (8, 1)).astype(np.uint16)


def unstriped(offs):
    return offs[:16].T.reshape(-1).astype(np.int64)

def planes(y):
    n, m = y.shape
    v = y.astype(np.float32).astype(ml_dtypes.bfloat16).astype(np.float64).reshape(n // 32, 32, m)
    top = np.abs(v).max(1)
    byte = np.clip(np.where(top > 0, np.frexp(top)[1] - 1 + 127 - 7, 1), 1, 254)
    codes = (v * np.exp2(127.0 - byte)[:, None, :]).reshape(n, m).astype(np.float32).astype(ml_dtypes.float8_e4m3fn).view(np.uint8)
    words = codes.reshape(n // 512, 128, 4, m).transpose(0, 1, 3, 2)
    return np.ascontiguousarray(words), np.ascontiguousarray(byte.astype(np.uint8).reshape(n // 512, 16, m))


K, T, S, V, N = 512, 4096, 1024, 512, 512


def setup_inputs():
    n = np.random.standard_normal
    s = mx_kscale(K)[:, None]
    return {
        "xT": (n((K, T)) * s).astype(np.float32),
        "sT": (n((K, V)) * s).astype(np.float32),
        "w1": (n((K, N)) / np.sqrt(K) / s).astype(np.float32),
        "w2": (n((K, N)) / np.sqrt(K) / s).astype(np.float32),
        "offs": striped(np.random.permutation(T)[:S]),
        "par": striped(np.random.randint(0, V, S)),
    }


def reference(xT, sT, w1, w2, offs, par):
    xq = mxq(f64(xT)[:, unstriped(offs)], 0, "e4m3")
    y = mxq(f64(w1), 0, "e4m3").T @ xq
    t = mxq(f64(w2), 0, "e4m3").T @ mxq(f64(sT), 0, "e4m3")
    out_0 = y + t[:, unstriped(par)]
    return (out_0,) + planes(out_0)

@@ -1,0 +1,165 @@
+from contextlib import ExitStack
+
+import concourse.mybir as mybir
+
+K, T, S, V, N = 512, 4096, 1024, 512, 512
+FLOPS = 2 * K * N * (S + V)
+
+F32 = mybir.dt.float32
+BF16 = mybir.dt.bfloat16
+I32 = mybir.dt.int32
+U32 = mybir.dt.uint32
+U16 = mybir.dt.uint16
+U8 = mybir.dt.uint8
+FP8X4 = mybir.dt.float8_e4m3fn_x4
+COPY = mybir.ActivationFunctionType.Copy
+ADD = mybir.AluOpType.add
+
+P = 128
+PACK = 4
+HALF = S // 2
+CHUNK = 256
+STEP = 128
+SPARE = 16
+
+
+def flat(tile):
+    return tile.rearrange("p c j -> p (c j)")
+
+
+def weave(copy, grouped, planes):
+    copy(
+        out=grouped.rearrange("p (c i) j -> p c j i", i=4),
+        in_=planes.rearrange("p j (c i) -> p c j i", i=4),
+    )
+
+
+def deal(copy, grouped, raw, first):
+    count = raw.shape[2] // PACK
+    copy(
+        out=grouped[:, :, first : first + count, :].rearrange("p t m j -> p m j t"),
+        in_=raw.rearrange("p j (m t) -> p m j t", t=PACK),
+    )
+
+
+def tile_picked_fpn_none_lo_kernel(tc, xT, sT, w1, w2, offs, par, out_0, out_1, out_2):
+    nc = tc.nc
+    with ExitStack() as ctx:
+        keep = ctx.enter_context(tc.tile_pool(name="keep", bufs=1))
+        psum = ctx.enter_context(tc.psum_pool(name="psum", bufs=8))
+
+        def quantize(codes, scales, grouped):
+            nc.vector.quantize_mx(out=codes.bitcast(FP8X4), scales=scales, in_=grouped)
+
+        def product(acc, w_codes, w_scales, t, codes, scales):
+            cols = slice(t * P, (t + 1) * P)
+            nc.tensor.matmul_mx(
+                out=acc,
+                lhsT=w_codes[:, cols].bitcast(FP8X4),
+                lhsT_scale=w_scales[:, cols],
+                rhs=codes.bitcast(FP8X4),
+                rhs_scale=scales,
+                start=True,
+                stop=True,
+            )
+
+        w2_raw = keep.tile([P, PACK, N], F32, name="w2_raw")
+        nc.sync.dma_start(out=w2_raw[:], in_=w2.rearrange("(p j) c -> p j c", j=PACK))
+        s_rows = sT.rearrange("(p j) v -> p j v", j=PACK)
+        s_raw = []
+        for h in range(2):
+            raw = keep.tile([P, PACK, V // 2], F32, name=f"s_raw{h}")
+            nc.sync.dma_start(out=raw[:], in_=s_rows[:, :, h * (V // 2) : (h + 1) * (V // 2)])
+            s_raw.append(raw)
+        parents = keep.tile([P, S // 16], U16, name="parents")
+        nc.sync.dma_start(parents[:], par)
+        picked = keep.tile([P, S // 16], U16, name="picked")
+        nc.sync.dma_start(picked[:], offs)
+        x_rows = xT.rearrange("(p j) c -> p j c", j=PACK)
+        x_raw = []
+        for j in range(PACK):
+            raw = keep.tile([P, T], F32, name=f"x_raw{j}")
+            nc.sync.dma_start(out=raw[:], in_=x_rows[:, j, :])
+            x_raw.append(raw)
+        w1_rows = w1.rearrange("(p j) c -> p j c", j=PACK)
+        w1_raw = []
+        for h in range(2):
+            raw = keep.tile([P, PACK, N // 2], F32, name=f"w1_raw{h}")
+            nc.sync.dma_start(out=raw[:], in_=w1_rows[:, :, h * (N // 2) : (h + 1) * (N // 2)])
+            w1_raw.append(raw)
+
+        w2_grouped = keep.tile([P, PACK, P, PACK], BF16, name="w2_grouped", align_bytes=64)
+        deal(nc.vector.tensor_copy, w2_grouped, w2_raw[:], 0)
+        w2_codes = keep.tile([P, N], U32, name="w2_codes", align_bytes=64)
+        w2_scales = keep.tile([P, N], U8, name="w2_scales", align_bytes=64)
+        quantize(w2_codes[:], w2_scales[:], w2_grouped[:].rearrange("p t m j -> p (t m j)"))
+        s_codes = keep.tile([P, V], U32, name="s_codes", align_bytes=64)
+        s_scales = keep.tile([P, V], U8, name="s_scales", align_bytes=64)
+        coarse = [keep.tile([P, V + SPARE], F32, name=f"coarse{t}") for t in range(PACK)]
+        for t in range(PACK):
+            nc.gpsimd.memset(coarse[t][:, V:], 0.0)
+        for h, copy in enumerate((nc.scalar.copy, nc.vector.tensor_copy)):
+            grouped = keep.tile([P, V // 2, PACK], BF16, name=f"s_grouped{h}", align_bytes=64)
+            weave(copy, grouped[:], s_raw[h][:])
+            cols = slice(h * (V // 2), (h + 1) * (V // 2))
+            quantize(s_codes[:, cols], s_scales[:, cols], flat(grouped[:]))
+            for t in range(PACK):
+                acc = psum.tile([P, V // 2], F32, name="acc")
+                product(acc[:], w2_codes, w2_scales, t, s_codes[:, cols], s_scales[:, cols])
+                nc.scalar.copy(out=coarse[t][:, cols], in_=acc[:])
+
+        fetched = keep.tile([P, PACK, S], F32, name="fetched")
+        for t in range(PACK):
+            for h in range(2):
+                entries = parents[:, h * (HALF // 16) : (h + 1) * (HALF // 16)]
+                nc.vector.tensor_copy(fetched[:, t, h * HALF : (h + 1) * HALF], coarse[t][:].indirect(entries))
+
+        x_grouped = keep.tile([P, S, PACK], BF16, name="x_grouped", align_bytes=64)
+        x0_cast = keep.tile([P, T], BF16, name="x0_cast")
+        nc.scalar.copy(out=x0_cast[:], in_=x_raw[0][:])
+        nc.scalar.activation(x_grouped[:, :, 0], x0_cast[:].indirect(picked[:]), COPY)
+        x1_picked = keep.tile([P, S], BF16, name="x1_picked")
+        nc.vector.tensor_copy(x1_picked[:], x_raw[1][:].indirect(picked[:]))
+        nc.scalar.copy(out=x_grouped[:, :, 1], in_=x1_picked[:])
+        nc.vector.tensor_copy(x_grouped[:, :, 2], x_raw[2][:].indirect(picked[:]))
+        x_codes = keep.tile([P, S], U32, name="x_codes", align_bytes=64)
+        x_scales = keep.tile([P, S], U8, name="x_scales", align_bytes=64)
+        for h in range(2):
+            cols = slice(h * HALF, (h + 1) * HALF)
+            entries = picked[:, h * (HALF // 16) : (h + 1) * (HALF // 16)]
+            nc.vector.tensor_copy(x_grouped[:, cols, 3], x_raw[3][:].indirect(entries))
+        for h in range(2):
+            cols = slice(h * HALF, (h + 1) * HALF)
+            quantize(x_codes[:, cols], x_scales[:, cols], flat(x_grouped[:, cols, :]))
+
+        w1_grouped = keep.tile([P, PACK, P, PACK], BF16, name="w1_grouped", align_bytes=64)
+        for h in range(2):
+            deal(nc.scalar.copy, w1_grouped, w1_raw[h][:], h * (P // 2))
+        w1_codes = keep.tile([P, N], U32, name="w1_codes", align_bytes=64)
+        w1_scales = keep.tile([P, N], U8, name="w1_scales", align_bytes=64)
+        for t in range(PACK):
+            cols = slice(t * P, (t + 1) * P)
+            quantize(w1_codes[:, cols], w1_scales[:, cols], flat(w1_grouped[:, t, :, :]))
+
+        out_rows = out_0.rearrange("(p t) c -> p t c", t=PACK)
+        out_words = out_1[0].rearrange("p c j -> p (c j)").bitcast(I32)
+        y_codes = keep.tile([P, S], U32, name="y_codes", align_bytes=64)
+        y_scales = keep.tile([P, S], U8, name="y_scales", align_bytes=64)
+        for c in range(S // CHUNK):
+            result = keep.tile([P, PACK, CHUNK], F32, name=f"result{c}")
+            for u in range(CHUNK // STEP):
+                part = slice(u * STEP, (u + 1) * STEP)
+                cols = slice(c * CHUNK + u * STEP, c * CHUNK + (u + 1) * STEP)
+                acc = psum.tile([P, PACK, STEP], F32, name="acc")
+                for t in range(PACK):
+                    product(acc[:, t, :], w1_codes, w1_scales, t, x_codes[:, cols], x_scales[:, cols])
+                nc.vector.tensor_tensor(result[:, :, part], acc[:], fetched[:, :, cols], ADD)
+                grouped = keep.tile([P, STEP, PACK], BF16, name=f"y_grouped{c}_{u}", align_bytes=64)
+                weave(nc.scalar.copy, grouped[:], result[:, :, part])
+                quantize(y_codes[:, cols], y_scales[:, cols], flat(grouped[:]))
+            cols = slice(c * CHUNK, (c + 1) * CHUNK)
+            nc.sync.dma_start(out=out_rows[:, :, cols], in_=result[:])
+            nc.sync.dma_start(out=out_words[:, cols], in_=y_codes[:, cols].bitcast(I32))
+        scale_rows = out_2[0].bitcast(I32)
+        for q, queue in enumerate((nc.scalar, nc.scalar, nc.sync, nc.sync)):
+            queue.dma_start(out=scale_rows[4 * q : 4 * q + 4, :], in_=y_scales[32 * q : 32 * q + 4, :].bitcast(I32))

@@ -19,7 +19,6 @@ P = 128
 PACK = 4
 HALF = S // 2
 CHUNK = 256
-STEP = 128
 SPARE = 16
 
 
@@ -65,12 +64,8 @@ def tile_picked_fpn_none_lo_kernel(tc, xT, sT, w1, w2, offs, par, out_0, out_1, 
 
         w2_raw = keep.tile([P, PACK, N], F32, name="w2_raw")
         nc.sync.dma_start(out=w2_raw[:], in_=w2.rearrange("(p j) c -> p j c", j=PACK))
-        s_rows = sT.rearrange("(p j) v -> p j v", j=PACK)
-        s_raw = []
-        for h in range(2):
-            raw = keep.tile([P, PACK, V // 2], F32, name=f"s_raw{h}")
-            nc.sync.dma_start(out=raw[:], in_=s_rows[:, :, h * (V // 2) : (h + 1) * (V // 2)])
-            s_raw.append(raw)
+        s_raw = keep.tile([P, PACK, V], F32, name="s_raw")
+        nc.sync.dma_start(out=s_raw[:], in_=sT.rearrange("(p j) v -> p j v", j=PACK))
         parents = keep.tile([P, S // 16], U16, name="parents")
         nc.sync.dma_start(parents[:], par)
         picked = keep.tile([P, S // 16], U16, name="picked")
@@ -98,10 +93,10 @@ def tile_picked_fpn_none_lo_kernel(tc, xT, sT, w1, w2, offs, par, out_0, out_1, 
         coarse = [keep.tile([P, V + SPARE], F32, name=f"coarse{t}") for t in range(PACK)]
         for t in range(PACK):
             nc.gpsimd.memset(coarse[t][:, V:], 0.0)
-        for h, copy in enumerate((nc.scalar.copy, nc.vector.tensor_copy)):
+        for h, copy in enumerate((nc.vector.tensor_copy, nc.scalar.copy)):
             grouped = keep.tile([P, V // 2, PACK], BF16, name=f"s_grouped{h}", align_bytes=64)
-            weave(copy, grouped[:], s_raw[h][:])
             cols = slice(h * (V // 2), (h + 1) * (V // 2))
+            weave(copy, grouped[:], s_raw[:, :, cols])
             quantize(s_codes[:, cols], s_scales[:, cols], flat(grouped[:]))
             for t in range(PACK):
                 acc = psum.tile([P, V // 2], F32, name="acc")
@@ -145,21 +140,28 @@ def tile_picked_fpn_none_lo_kernel(tc, xT, sT, w1, w2, offs, par, out_0, out_1, 
         out_words = out_1[0].rearrange("p c j -> p (c j)").bitcast(I32)
         y_codes = keep.tile([P, S], U32, name="y_codes", align_bytes=64)
         y_scales = keep.tile([P, S], U8, name="y_scales", align_bytes=64)
+        results = []
+        for h in range(2):
+            cols = slice(h * HALF, (h + 1) * HALF)
+            result = keep.tile([P, PACK, HALF], F32, name=f"result{h}")
+            results.append(result)
+            for t in range(PACK):
+                acc = psum.tile([P, HALF], F32, name="acc")
+                product(acc[:], w1_codes, w1_scales, t, x_codes[:, cols], x_scales[:, cols])
+                nc.vector.tensor_tensor(result[:, t, :], acc[:], fetched[:, t, cols], ADD)
+                nc.sync.dma_start(out=out_rows[:, t, cols], in_=result[:, t, :])
+        copies = (nc.scalar.copy, nc.scalar.copy, nc.scalar.copy, nc.vector.tensor_copy)
+        y_grouped = []
+        for c, copy in enumerate(copies):
+            grouped = keep.tile([P, CHUNK, PACK], BF16, name=f"y_grouped{c}", align_bytes=64)
+            weave(copy, grouped[:], results[c // 2][:, :, (c % 2) * CHUNK : (c % 2 + 1) * CHUNK])
+            y_grouped.append(grouped)
         for c in range(S // CHUNK):
-            result = keep.tile([P, PACK, CHUNK], F32, name=f"result{c}")
-            for u in range(CHUNK // STEP):
-                part = slice(u * STEP, (u + 1) * STEP)
-                cols = slice(c * CHUNK + u * STEP, c * CHUNK + (u + 1) * STEP)
-                acc = psum.tile([P, PACK, STEP], F32, name="acc")
-                for t in range(PACK):
-                    product(acc[:, t, :], w1_codes, w1_scales, t, x_codes[:, cols], x_scales[:, cols])
-                nc.vector.tensor_tensor(result[:, :, part], acc[:], fetched[:, :, cols], ADD)
-                grouped = keep.tile([P, STEP, PACK], BF16, name=f"y_grouped{c}_{u}", align_bytes=64)
-                weave(nc.scalar.copy, grouped[:], result[:, :, part])
-                quantize(y_codes[:, cols], y_scales[:, cols], flat(grouped[:]))
             cols = slice(c * CHUNK, (c + 1) * CHUNK)
-            nc.sync.dma_start(out=out_rows[:, :, cols], in_=result[:])
-            nc.sync.dma_start(out=out_words[:, cols], in_=y_codes[:, cols].bitcast(I32))
+            quantize(y_codes[:, cols], y_scales[:, cols], flat(y_grouped[c][:]))
+            if c % 2:
+                cols = slice((c - 1) * CHUNK, (c + 1) * CHUNK)
+                nc.sync.dma_start(out=out_words[:, cols], in_=y_codes[:, cols].bitcast(I32))
         scale_rows = out_2[0].bitcast(I32)
         for q, queue in enumerate((nc.scalar, nc.scalar, nc.sync, nc.sync)):
             queue.dma_start(out=scale_rows[4 * q : 4 * q + 4, :], in_=y_scales[32 * q : 32 * q + 4, :].bitcast(I32))

@@ -79,7 +79,7 @@ def tile_picked_fpn_none_lo_kernel(tc, xT, sT, w1, w2, offs, par, out_0, out_1, 
         w1_rows = w1.rearrange("(p j) c -> p j c", j=PACK)
         w1_raw = []
         for h in range(2):
-            raw = keep.tile([P, PACK, N // 2], F32, name=f"w1_raw{h}")
+            raw = keep.tile([P, PACK, N // 2], F32, name=f"w1_raw{h}", tag=f"late{h}", align_bytes=64)
             nc.sync.dma_start(out=raw[:], in_=w1_rows[:, :, h * (N // 2) : (h + 1) * (N // 2)])
             w1_raw.append(raw)
 
@@ -98,7 +98,9 @@ def tile_picked_fpn_none_lo_kernel(tc, xT, sT, w1, w2, offs, par, out_0, out_1, 
             cols = slice(h * (V // 2), (h + 1) * (V // 2))
             weave(copy, grouped[:], s_raw[:, :, cols])
             quantize(s_codes[:, cols], s_scales[:, cols], flat(grouped[:]))
-            for t in range(PACK):
+        for t in range(PACK):
+            for h in range(2):
+                cols = slice(h * (V // 2), (h + 1) * (V // 2))
                 acc = psum.tile([P, V // 2], F32, name="acc")
                 product(acc[:], w2_codes, w2_scales, t, s_codes[:, cols], s_scales[:, cols])
                 nc.scalar.copy(out=coarse[t][:, cols], in_=acc[:])
@@ -109,23 +111,21 @@ def tile_picked_fpn_none_lo_kernel(tc, xT, sT, w1, w2, offs, par, out_0, out_1, 
                 entries = parents[:, h * (HALF // 16) : (h + 1) * (HALF // 16)]
                 nc.vector.tensor_copy(fetched[:, t, h * HALF : (h + 1) * HALF], coarse[t][:].indirect(entries))
 
-        x_grouped = keep.tile([P, S, PACK], BF16, name="x_grouped", align_bytes=64)
+        halves = [slice(h * HALF, (h + 1) * HALF) for h in range(2)]
+        entries = [picked[:, h * (HALF // 16) : (h + 1) * (HALF // 16)] for h in range(2)]
+        x_picked = keep.tile([P, PACK, S], BF16, name="x_picked")
+        x_first = keep.tile([P, HALF, PACK], BF16, name="x_first", align_bytes=64)
         x0_cast = keep.tile([P, T], BF16, name="x0_cast")
         nc.scalar.copy(out=x0_cast[:], in_=x_raw[0][:])
-        nc.scalar.activation(x_grouped[:, :, 0], x0_cast[:].indirect(picked[:]), COPY)
-        x1_picked = keep.tile([P, S], BF16, name="x1_picked")
-        nc.vector.tensor_copy(x1_picked[:], x_raw[1][:].indirect(picked[:]))
-        nc.scalar.copy(out=x_grouped[:, :, 1], in_=x1_picked[:])
-        nc.vector.tensor_copy(x_grouped[:, :, 2], x_raw[2][:].indirect(picked[:]))
+        nc.scalar.activation(x_picked[:, 0, :], x0_cast[:].indirect(picked[:]), COPY)
+        nc.vector.tensor_copy(x_picked[:, 1, :], x_raw[1][:].indirect(picked[:]))
+        weave(nc.scalar.copy, x_first[:, :, 0:2], x_picked[:, 0:2, halves[0]])
+        for j in (2, 3):
+            nc.vector.tensor_copy(x_first[:, :, j], x_raw[j][:].indirect(entries[0]))
+            nc.vector.tensor_copy(x_picked[:, j, halves[1]], x_raw[j][:].indirect(entries[1]))
         x_codes = keep.tile([P, S], U32, name="x_codes", align_bytes=64)
         x_scales = keep.tile([P, S], U8, name="x_scales", align_bytes=64)
-        for h in range(2):
-            cols = slice(h * HALF, (h + 1) * HALF)
-            entries = picked[:, h * (HALF // 16) : (h + 1) * (HALF // 16)]
-            nc.vector.tensor_copy(x_grouped[:, cols, 3], x_raw[3][:].indirect(entries))
-        for h in range(2):
-            cols = slice(h * HALF, (h + 1) * HALF)
-            quantize(x_codes[:, cols], x_scales[:, cols], flat(x_grouped[:, cols, :]))
+        quantize(x_codes[:, halves[0]], x_scales[:, halves[0]], flat(x_first[:]))
 
         w1_grouped = keep.tile([P, PACK, P, PACK], BF16, name="w1_grouped", align_bytes=64)
         for h in range(2):
@@ -135,6 +135,12 @@ def tile_picked_fpn_none_lo_kernel(tc, xT, sT, w1, w2, offs, par, out_0, out_1, 
         for t in range(PACK):
             cols = slice(t * P, (t + 1) * P)
             quantize(w1_codes[:, cols], w1_scales[:, cols], flat(w1_grouped[:, t, :, :]))
+        x_second = keep.tile([P, HALF, PACK], BF16, name="x_second", tag="late1", align_bytes=64)
+        for c in range(2):
+            part = slice(c * CHUNK, (c + 1) * CHUNK)
+            cols = slice(HALF + c * CHUNK, HALF + (c + 1) * CHUNK)
+            weave(nc.scalar.copy, x_second[:, part, :], x_picked[:, :, cols])
+            quantize(x_codes[:, cols], x_scales[:, cols], flat(x_second[:, part, :]))
 
         out_rows = out_0.rearrange("(p t) c -> p t c", t=PACK)
         out_words = out_1[0].rearrange("p c j -> p (c j)").bitcast(I32)

@@ -14,12 +14,14 @@ U8 = mybir.dt.uint8
 FP8X4 = mybir.dt.float8_e4m3fn_x4
 COPY = mybir.ActivationFunctionType.Copy
 ADD = mybir.AluOpType.add
+MULT = mybir.AluOpType.mult
 
 P = 128
 PACK = 4
 HALF = S // 2
 CHUNK = 256
 SPARE = 16
+SHARE = 96
 
 
 def flat(tile):
@@ -146,22 +148,28 @@ def tile_picked_fpn_none_lo_kernel(tc, xT, sT, w1, w2, offs, par, out_0, out_1, 
         out_words = out_1[0].rearrange("p c j -> p (c j)").bitcast(I32)
         y_codes = keep.tile([P, S], U32, name="y_codes", align_bytes=64)
         y_scales = keep.tile([P, S], U8, name="y_scales", align_bytes=64)
-        results = []
-        for h in range(2):
-            cols = slice(h * HALF, (h + 1) * HALF)
-            result = keep.tile([P, PACK, HALF], F32, name=f"result{h}")
-            results.append(result)
-            for t in range(PACK):
-                acc = psum.tile([P, HALF], F32, name="acc")
-                product(acc[:], w1_codes, w1_scales, t, x_codes[:, cols], x_scales[:, cols])
-                nc.vector.tensor_tensor(result[:, t, :], acc[:], fetched[:, t, cols], ADD)
-                nc.sync.dma_start(out=out_rows[:, t, cols], in_=result[:, t, :])
-        copies = (nc.scalar.copy, nc.scalar.copy, nc.scalar.copy, nc.vector.tensor_copy)
-        y_grouped = []
-        for c, copy in enumerate(copies):
-            grouped = keep.tile([P, CHUNK, PACK], BF16, name=f"y_grouped{c}", align_bytes=64)
-            weave(copy, grouped[:], results[c // 2][:, :, (c % 2) * CHUNK : (c % 2 + 1) * CHUNK])
-            y_grouped.append(grouped)
+        results = [keep.tile([P, PACK, HALF], F32, name=f"result{h}") for h in range(2)]
+        for t in range(PACK):
+            acc = psum.tile([P, HALF], F32, name="acc")
+            product(acc[:], w1_codes, w1_scales, t, x_codes[:, halves[0]], x_scales[:, halves[0]])
+            nc.vector.tensor_tensor(results[0][:, t, :], acc[:], fetched[:, t, halves[0]], ADD)
+            nc.sync.dma_start(out=out_rows[:, t, halves[0]], in_=results[0][:, t, :])
+        for c in range(2):
+            part = slice(c * CHUNK, (c + 1) * CHUNK)
+            cols = slice(HALF + c * CHUNK, HALF + (c + 1) * CHUNK)
+            for a in range(2):
+                pair = slice(2 * a, 2 * a + 2)
+                acc = psum.tile([P, 2, CHUNK], F32, name="acc")
+                for u in range(2):
+                    product(acc[:, u, :], w1_codes, w1_scales, 2 * a + u, x_codes[:, cols], x_scales[:, cols])
+                nc.vector.tensor_tensor(results[1][:, pair, part], acc[:], fetched[:, pair, cols], ADD)
+                nc.sync.dma_start(out=out_rows[:, pair, cols], in_=results[1][:, pair, part])
+        y_grouped = [keep.tile([P, CHUNK, PACK], BF16, name=f"y_grouped{c}", align_bytes=64) for c in range(S // CHUNK)]
+        weave(nc.scalar.copy, y_grouped[0][:], results[0][:, :, :CHUNK])
+        nc.gpsimd.tensor_scalar(y_grouped[1][:], results[0][:, :, CHUNK:].rearrange("p j c -> p c j"), 1.0, 0.0, MULT, ADD)
+        weave(nc.scalar.copy, y_grouped[2][:], results[1][:, :, :CHUNK])
+        weave(nc.scalar.copy, y_grouped[3][:, :SHARE, :], results[1][:, :, CHUNK : CHUNK + SHARE])
+        weave(nc.vector.tensor_copy, y_grouped[3][:, SHARE:, :], results[1][:, :, CHUNK + SHARE :])
         for c in range(S // CHUNK):
             cols = slice(c * CHUNK, (c + 1) * CHUNK)
             quantize(y_codes[:, cols], y_scales[:, cols], flat(y_grouped[c][:]))

@@ -22,6 +22,7 @@ HALF = S // 2
 CHUNK = 256
 SPARE = 16
 SHARE = 96
+CUTS = ((0, 128), (128, 256), (256, 384), (384, 512))
 
 
 def flat(tile):
@@ -80,9 +81,9 @@ def tile_picked_fpn_none_lo_kernel(tc, xT, sT, w1, w2, offs, par, out_0, out_1, 
             x_raw.append(raw)
         w1_rows = w1.rearrange("(p j) c -> p j c", j=PACK)
         w1_raw = []
-        for h in range(2):
-            raw = keep.tile([P, PACK, N // 2], F32, name=f"w1_raw{h}", tag=f"late{h}", align_bytes=64)
-            nc.sync.dma_start(out=raw[:], in_=w1_rows[:, :, h * (N // 2) : (h + 1) * (N // 2)])
+        for h, (first, last) in enumerate(CUTS):
+            raw = keep.tile([P, PACK, last - first], F32, name=f"w1_raw{h}", tag=f"late{h}", align_bytes=64)
+            nc.sync.dma_start(out=raw[:], in_=w1_rows[:, :, first:last])
             w1_raw.append(raw)
 
         w2_grouped = keep.tile([P, PACK, P, PACK], BF16, name="w2_grouped", align_bytes=64)
@@ -120,7 +121,9 @@ def tile_picked_fpn_none_lo_kernel(tc, xT, sT, w1, w2, offs, par, out_0, out_1, 
         x0_cast = keep.tile([P, T], BF16, name="x0_cast")
         nc.scalar.copy(out=x0_cast[:], in_=x_raw[0][:])
         nc.scalar.activation(x_picked[:, 0, :], x0_cast[:].indirect(picked[:]), COPY)
-        nc.vector.tensor_copy(x_picked[:, 1, :], x_raw[1][:].indirect(picked[:]))
+        x1_cast = keep.tile([P, T], BF16, name="x1_cast")
+        nc.gpsimd.tensor_scalar(x1_cast[:], x_raw[1][:], 1.0, 0.0, MULT, ADD)
+        nc.scalar.activation(x_picked[:, 1, :], x1_cast[:].indirect(picked[:]), COPY)
         weave(nc.scalar.copy, x_first[:, :, 0:2], x_picked[:, 0:2, halves[0]])
         for j in (2, 3):
             nc.vector.tensor_copy(x_first[:, :, j], x_raw[j][:].indirect(entries[0]))
@@ -130,14 +133,14 @@ def tile_picked_fpn_none_lo_kernel(tc, xT, sT, w1, w2, offs, par, out_0, out_1, 
         quantize(x_codes[:, halves[0]], x_scales[:, halves[0]], flat(x_first[:]))
 
         w1_grouped = keep.tile([P, PACK, P, PACK], BF16, name="w1_grouped", align_bytes=64)
-        for h in range(2):
-            deal(nc.scalar.copy, w1_grouped, w1_raw[h][:], h * (P // 2))
+        for h, (first, last) in enumerate(CUTS):
+            deal(nc.scalar.copy, w1_grouped, w1_raw[h][:], first // PACK)
         w1_codes = keep.tile([P, N], U32, name="w1_codes", align_bytes=64)
         w1_scales = keep.tile([P, N], U8, name="w1_scales", align_bytes=64)
         for t in range(PACK):
             cols = slice(t * P, (t + 1) * P)
             quantize(w1_codes[:, cols], w1_scales[:, cols], flat(w1_grouped[:, t, :, :]))
-        x_second = keep.tile([P, HALF, PACK], BF16, name="x_second", tag="late1", align_bytes=64)
+        x_second = keep.tile([P, HALF, PACK], BF16, name="x_second", tag="late3", align_bytes=64)
         for c in range(2):
             part = slice(c * CHUNK, (c + 1) * CHUNK)
             cols = slice(HALF + c * CHUNK, HALF + (c + 1) * CHUNK)

@@ -121,9 +121,7 @@ def tile_picked_fpn_none_lo_kernel(tc, xT, sT, w1, w2, offs, par, out_0, out_1, 
         x0_cast = keep.tile([P, T], BF16, name="x0_cast")
         nc.scalar.copy(out=x0_cast[:], in_=x_raw[0][:])
         nc.scalar.activation(x_picked[:, 0, :], x0_cast[:].indirect(picked[:]), COPY)
-        x1_cast = keep.tile([P, T], BF16, name="x1_cast")
-        nc.gpsimd.tensor_scalar(x1_cast[:], x_raw[1][:], 1.0, 0.0, MULT, ADD)
-        nc.scalar.activation(x_picked[:, 1, :], x1_cast[:].indirect(picked[:]), COPY)
+        nc.vector.tensor_copy(x_picked[:, 1, :], x_raw[1][:].indirect(picked[:]))
         weave(nc.scalar.copy, x_first[:, :, 0:2], x_picked[:, 0:2, halves[0]])
         for j in (2, 3):
             nc.vector.tensor_copy(x_first[:, :, j], x_raw[j][:].indirect(entries[0]))

@@ -21,7 +21,7 @@ PACK = 4
 HALF = S // 2
 CHUNK = 256
 SPARE = 16
-SHARE = 96
+SHARE = 128
 CUTS = ((0, 128), (128, 256), (256, 384), (384, 512))
 
 
@@ -135,9 +135,9 @@ def tile_picked_fpn_none_lo_kernel(tc, xT, sT, w1, w2, offs, par, out_0, out_1, 
             deal(nc.scalar.copy, w1_grouped, w1_raw[h][:], first // PACK)
         w1_codes = keep.tile([P, N], U32, name="w1_codes", align_bytes=64)
         w1_scales = keep.tile([P, N], U8, name="w1_scales", align_bytes=64)
-        for t in range(PACK):
-            cols = slice(t * P, (t + 1) * P)
-            quantize(w1_codes[:, cols], w1_scales[:, cols], flat(w1_grouped[:, t, :, :]))
+        for first, last in ((0, 1), (1, 2), (2, 4)):
+            cols = slice(first * P, last * P)
+            quantize(w1_codes[:, cols], w1_scales[:, cols], w1_grouped[:, first:last, :, :].rearrange("p t m j -> p (t m j)"))
         x_second = keep.tile([P, HALF, PACK], BF16, name="x_second", tag="late3", align_bytes=64)
         for c in range(2):
             part = slice(c * CHUNK, (c + 1) * CHUNK)
@@ -151,9 +151,12 @@ def tile_picked_fpn_none_lo_kernel(tc, xT, sT, w1, w2, offs, par, out_0, out_1, 
         y_scales = keep.tile([P, S], U8, name="y_scales", align_bytes=64)
         results = [keep.tile([P, PACK, HALF], F32, name=f"result{h}") for h in range(2)]
         for t in range(PACK):
-            acc = psum.tile([P, HALF], F32, name="acc")
-            product(acc[:], w1_codes, w1_scales, t, x_codes[:, halves[0]], x_scales[:, halves[0]])
-            nc.vector.tensor_tensor(results[0][:, t, :], acc[:], fetched[:, t, halves[0]], ADD)
+            width = CHUNK if t == 0 else HALF
+            for first in range(0, HALF, width):
+                cols = slice(first, first + width)
+                acc = psum.tile([P, width], F32, name="acc")
+                product(acc[:], w1_codes, w1_scales, t, x_codes[:, cols], x_scales[:, cols])
+                nc.vector.tensor_tensor(results[0][:, t, cols], acc[:], fetched[:, t, cols], ADD)
             nc.sync.dma_start(out=out_rows[:, t, halves[0]], in_=results[0][:, t, :])
         for c in range(2):
             part = slice(c * CHUNK, (c + 1) * CHUNK)
@@ -165,18 +168,19 @@ def tile_picked_fpn_none_lo_kernel(tc, xT, sT, w1, w2, offs, par, out_0, out_1, 
                     product(acc[:, u, :], w1_codes, w1_scales, 2 * a + u, x_codes[:, cols], x_scales[:, cols])
                 nc.vector.tensor_tensor(results[1][:, pair, part], acc[:], fetched[:, pair, cols], ADD)
                 nc.sync.dma_start(out=out_rows[:, pair, cols], in_=results[1][:, pair, part])
-        y_grouped = [keep.tile([P, CHUNK, PACK], BF16, name=f"y_grouped{c}", align_bytes=64) for c in range(S // CHUNK)]
-        weave(nc.scalar.copy, y_grouped[0][:], results[0][:, :, :CHUNK])
-        nc.gpsimd.tensor_scalar(y_grouped[1][:], results[0][:, :, CHUNK:].rearrange("p j c -> p c j"), 1.0, 0.0, MULT, ADD)
-        weave(nc.scalar.copy, y_grouped[2][:], results[1][:, :, :CHUNK])
-        weave(nc.scalar.copy, y_grouped[3][:, :SHARE, :], results[1][:, :, CHUNK : CHUNK + SHARE])
-        weave(nc.vector.tensor_copy, y_grouped[3][:, SHARE:, :], results[1][:, :, CHUNK + SHARE :])
-        for c in range(S // CHUNK):
-            cols = slice(c * CHUNK, (c + 1) * CHUNK)
-            quantize(y_codes[:, cols], y_scales[:, cols], flat(y_grouped[c][:]))
-            if c % 2:
-                cols = slice((c - 1) * CHUNK, (c + 1) * CHUNK)
-                nc.sync.dma_start(out=out_words[:, cols], in_=y_codes[:, cols].bitcast(I32))
+        y_first = keep.tile([P, HALF, PACK], BF16, name="y_first", align_bytes=64)
+        y_late = [keep.tile([P, CHUNK, PACK], BF16, name=f"y_late{c}", align_bytes=64) for c in range(2)]
+        weave(nc.scalar.copy, y_first[:, :CHUNK, :], results[0][:, :, :CHUNK])
+        nc.gpsimd.tensor_scalar(y_first[:, CHUNK:, :], results[0][:, :, CHUNK:].rearrange("p j c -> p c j"), 1.0, 0.0, MULT, ADD)
+        weave(nc.scalar.copy, y_late[0][:], results[1][:, :, :CHUNK])
+        weave(nc.scalar.copy, y_late[1][:, :SHARE, :], results[1][:, :, CHUNK : CHUNK + SHARE])
+        weave(nc.vector.tensor_copy, y_late[1][:, SHARE:, :], results[1][:, :, CHUNK + SHARE :])
+        quantize(y_codes[:, halves[0]], y_scales[:, halves[0]], flat(y_first[:]))
+        nc.sync.dma_start(out=out_words[:, halves[0]], in_=y_codes[:, halves[0]].bitcast(I32))
+        for c in range(2):
+            cols = slice(HALF + c * CHUNK, HALF + (c + 1) * CHUNK)
+            quantize(y_codes[:, cols], y_scales[:, cols], flat(y_late[c][:]))
+        nc.sync.dma_start(out=out_words[:, halves[1]], in_=y_codes[:, halves[1]].bitcast(I32))
         scale_rows = out_2[0].bitcast(I32)
         for q, queue in enumerate((nc.scalar, nc.scalar, nc.sync, nc.sync)):
             queue.dma_start(out=scale_rows[4 * q : 4 * q + 4, :], in_=y_scales[32 * q : 32 * q + 4, :].bitcast(I32))

@@ -21,7 +21,7 @@ PACK = 4
 HALF = S // 2
 CHUNK = 256
 SPARE = 16
-SHARE = 128
+SHARE = 64
 CUTS = ((0, 128), (128, 256), (256, 384), (384, 512))
 
 
@@ -158,16 +158,25 @@ def tile_picked_fpn_none_lo_kernel(tc, xT, sT, w1, w2, offs, par, out_0, out_1, 
                 product(acc[:], w1_codes, w1_scales, t, x_codes[:, cols], x_scales[:, cols])
                 nc.vector.tensor_tensor(results[0][:, t, cols], acc[:], fetched[:, t, cols], ADD)
             nc.sync.dma_start(out=out_rows[:, t, halves[0]], in_=results[0][:, t, :])
-        for c in range(2):
+        def wide(t):
+            acc = psum.tile([P, HALF], F32, name="acc")
+            product(acc[:], w1_codes, w1_scales, t, x_codes[:, halves[1]], x_scales[:, halves[1]])
+            nc.vector.tensor_tensor(results[1][:, t, :], acc[:], fetched[:, t, halves[1]], ADD)
+            nc.sync.dma_start(out=out_rows[:, t, halves[1]], in_=results[1][:, t, :])
+
+        def paired(c):
             part = slice(c * CHUNK, (c + 1) * CHUNK)
             cols = slice(HALF + c * CHUNK, HALF + (c + 1) * CHUNK)
-            for a in range(2):
-                pair = slice(2 * a, 2 * a + 2)
-                acc = psum.tile([P, 2, CHUNK], F32, name="acc")
-                for u in range(2):
-                    product(acc[:, u, :], w1_codes, w1_scales, 2 * a + u, x_codes[:, cols], x_scales[:, cols])
-                nc.vector.tensor_tensor(results[1][:, pair, part], acc[:], fetched[:, pair, cols], ADD)
-                nc.sync.dma_start(out=out_rows[:, pair, cols], in_=results[1][:, pair, part])
+            acc = psum.tile([P, 2, CHUNK], F32, name="acc")
+            for u in range(2):
+                product(acc[:, u, :], w1_codes, w1_scales, 2 + u, x_codes[:, cols], x_scales[:, cols])
+            nc.vector.tensor_tensor(results[1][:, 2:4, part], acc[:], fetched[:, 2:4, cols], ADD)
+            nc.sync.dma_start(out=out_rows[:, 2:4, cols], in_=results[1][:, 2:4, part])
+
+        paired(0)
+        wide(0)
+        wide(1)
+        paired(1)
         y_first = keep.tile([P, HALF, PACK], BF16, name="y_first", align_bytes=64)
         y_late = [keep.tile([P, CHUNK, PACK], BF16, name=f"y_late{c}", align_bytes=64) for c in range(2)]
         weave(nc.scalar.copy, y_first[:, :CHUNK, :], results[0][:, :, :CHUNK])

@@ -22,7 +22,6 @@ HALF = S // 2
 CHUNK = 256
 SPARE = 16
 SHARE = 64
-CUTS = ((0, 128), (128, 256), (256, 384), (384, 512))
 
 
 def flat(tile):
@@ -41,6 +40,13 @@ def deal(copy, grouped, raw, first):
     copy(
         out=grouped[:, :, first : first + count, :].rearrange("p t m j -> p m j t"),
         in_=raw.rearrange("p j (m t) -> p m j t", t=PACK),
+    )
+
+
+def deal_pair(copy, grouped, raw, first):
+    copy(
+        out=grouped.rearrange("p t m j -> p m j t"),
+        in_=raw.rearrange("p j (m t) -> p m j t", t=PACK)[:, :, :, first : first + 2],
     )
 
 
@@ -79,12 +85,8 @@ def tile_picked_fpn_none_lo_kernel(tc, xT, sT, w1, w2, offs, par, out_0, out_1, 
             raw = keep.tile([P, T], F32, name=f"x_raw{j}")
             nc.sync.dma_start(out=raw[:], in_=x_rows[:, j, :])
             x_raw.append(raw)
-        w1_rows = w1.rearrange("(p j) c -> p j c", j=PACK)
-        w1_raw = []
-        for h, (first, last) in enumerate(CUTS):
-            raw = keep.tile([P, PACK, last - first], F32, name=f"w1_raw{h}", tag=f"late{h}", align_bytes=64)
-            nc.sync.dma_start(out=raw[:], in_=w1_rows[:, :, first:last])
-            w1_raw.append(raw)
+        w1_raw = keep.tile([P, PACK, N], F32, name="w1_raw", tag="late", align_bytes=64)
+        nc.sync.dma_start(out=w1_raw[:], in_=w1.rearrange("(p j) c -> p j c", j=PACK))
 
         w2_grouped = keep.tile([P, PACK, P, PACK], BF16, name="w2_grouped", align_bytes=64)
         deal(nc.vector.tensor_copy, w2_grouped, w2_raw[:], 0)
@@ -118,32 +120,34 @@ def tile_picked_fpn_none_lo_kernel(tc, xT, sT, w1, w2, offs, par, out_0, out_1, 
         entries = [picked[:, h * (HALF // 16) : (h + 1) * (HALF // 16)] for h in range(2)]
         x_picked = keep.tile([P, PACK, S], BF16, name="x_picked")
         x_first = keep.tile([P, HALF, PACK], BF16, name="x_first", align_bytes=64)
-        x0_cast = keep.tile([P, T], BF16, name="x0_cast")
-        nc.scalar.copy(out=x0_cast[:], in_=x_raw[0][:])
-        nc.scalar.activation(x_picked[:, 0, :], x0_cast[:].indirect(picked[:]), COPY)
-        nc.vector.tensor_copy(x_picked[:, 1, :], x_raw[1][:].indirect(picked[:]))
+        for j in (0, 1):
+            nc.scalar.activation(x_picked[:, j, :], x_raw[j][:].indirect(picked[:]), COPY)
         weave(nc.scalar.copy, x_first[:, :, 0:2], x_picked[:, 0:2, halves[0]])
         for j in (2, 3):
             nc.vector.tensor_copy(x_first[:, :, j], x_raw[j][:].indirect(entries[0]))
-            nc.vector.tensor_copy(x_picked[:, j, halves[1]], x_raw[j][:].indirect(entries[1]))
-        x_codes = keep.tile([P, S], U32, name="x_codes", align_bytes=64)
+            nc.scalar.activation(x_picked[:, j, halves[1]], x_raw[j][:].indirect(entries[1]), COPY)
+        x_codes = [keep.tile([P, HALF], U32, name="x_codes0", align_bytes=64)]
         x_scales = keep.tile([P, S], U8, name="x_scales", align_bytes=64)
-        quantize(x_codes[:, halves[0]], x_scales[:, halves[0]], flat(x_first[:]))
+        quantize(x_codes[0][:], x_scales[:, halves[0]], flat(x_first[:]))
 
-        w1_grouped = keep.tile([P, PACK, P, PACK], BF16, name="w1_grouped", align_bytes=64)
-        for h, (first, last) in enumerate(CUTS):
-            deal(nc.scalar.copy, w1_grouped, w1_raw[h][:], first // PACK)
+        late = [slice(HALF + c * CHUNK, HALF + (c + 1) * CHUNK) for c in range(2)]
+        x_third = keep.tile([P, CHUNK, PACK], BF16, name="x_third", align_bytes=64)
+        weave(nc.scalar.copy, x_third[:], x_picked[:, :, late[0]])
+
+        w1_grouped = [keep.tile([P, 2, P, PACK], BF16, name=f"w1_grouped{u}", tag=f"dealt{u}", align_bytes=64) for u in range(2)]
+        deal_pair(nc.vector.tensor_copy, w1_grouped[0][:], w1_raw[:], 0)
+        deal_pair(nc.scalar.copy, w1_grouped[1][:], w1_raw[:], 2)
         w1_codes = keep.tile([P, N], U32, name="w1_codes", align_bytes=64)
         w1_scales = keep.tile([P, N], U8, name="w1_scales", align_bytes=64)
-        for first, last in ((0, 1), (1, 2), (2, 4)):
-            cols = slice(first * P, last * P)
-            quantize(w1_codes[:, cols], w1_scales[:, cols], w1_grouped[:, first:last, :, :].rearrange("p t m j -> p (t m j)"))
-        x_second = keep.tile([P, HALF, PACK], BF16, name="x_second", tag="late3", align_bytes=64)
-        for c in range(2):
-            part = slice(c * CHUNK, (c + 1) * CHUNK)
-            cols = slice(HALF + c * CHUNK, HALF + (c + 1) * CHUNK)
-            weave(nc.scalar.copy, x_second[:, part, :], x_picked[:, :, cols])
-            quantize(x_codes[:, cols], x_scales[:, cols], flat(x_second[:, part, :]))
+        for t in range(2):
+            cols = slice(t * P, (t + 1) * P)
+            quantize(w1_codes[:, cols], w1_scales[:, cols], flat(w1_grouped[0][:, t, :, :]))
+        x_codes.append(keep.tile([P, HALF], U32, name="x_codes1", tag="dealt0", align_bytes=64))
+        quantize(x_codes[1][:, :CHUNK], x_scales[:, late[0]], flat(x_third[:]))
+        quantize(w1_codes[:, 2 * P :], w1_scales[:, 2 * P :], w1_grouped[1][:].rearrange("p t m j -> p (t m j)"))
+        x_fourth = keep.tile([P, CHUNK, PACK], BF16, name="x_fourth", tag="late", align_bytes=64)
+        weave(nc.scalar.copy, x_fourth[:], x_picked[:, :, late[1]])
+        quantize(x_codes[1][:, CHUNK:], x_scales[:, late[1]], flat(x_fourth[:]))
 
         out_rows = out_0.rearrange("(p t) c -> p t c", t=PACK)
         out_words = out_1[0].rearrange("p c j -> p (c j)").bitcast(I32)
@@ -155,12 +159,12 @@ def tile_picked_fpn_none_lo_kernel(tc, xT, sT, w1, w2, offs, par, out_0, out_1, 
             for first in range(0, HALF, width):
                 cols = slice(first, first + width)
                 acc = psum.tile([P, width], F32, name="acc")
-                product(acc[:], w1_codes, w1_scales, t, x_codes[:, cols], x_scales[:, cols])
+                product(acc[:], w1_codes, w1_scales, t, x_codes[0][:, cols], x_scales[:, cols])
                 nc.vector.tensor_tensor(results[0][:, t, cols], acc[:], fetched[:, t, cols], ADD)
             nc.sync.dma_start(out=out_rows[:, t, halves[0]], in_=results[0][:, t, :])
         def wide(t):
             acc = psum.tile([P, HALF], F32, name="acc")
-            product(acc[:], w1_codes, w1_scales, t, x_codes[:, halves[1]], x_scales[:, halves[1]])
+            product(acc[:], w1_codes, w1_scales, t, x_codes[1][:], x_scales[:, halves[1]])
             nc.vector.tensor_tensor(results[1][:, t, :], acc[:], fetched[:, t, halves[1]], ADD)
             nc.sync.dma_start(out=out_rows[:, t, halves[1]], in_=results[1][:, t, :])
 
@@ -169,7 +173,7 @@ def tile_picked_fpn_none_lo_kernel(tc, xT, sT, w1, w2, offs, par, out_0, out_1, 
             cols = slice(HALF + c * CHUNK, HALF + (c + 1) * CHUNK)
             acc = psum.tile([P, 2, CHUNK], F32, name="acc")
             for u in range(2):
-                product(acc[:, u, :], w1_codes, w1_scales, 2 + u, x_codes[:, cols], x_scales[:, cols])
+                product(acc[:, u, :], w1_codes, w1_scales, 2 + u, x_codes[1][:, part], x_scales[:, cols])
             nc.vector.tensor_tensor(results[1][:, 2:4, part], acc[:], fetched[:, 2:4, cols], ADD)
             nc.sync.dma_start(out=out_rows[:, 2:4, cols], in_=results[1][:, 2:4, part])
 

@@ -21,7 +21,8 @@ PACK = 4
 HALF = S // 2
 CHUNK = 256
 SPARE = 16
-SHARE = 64
+SHARE = 144
+EARLY = 352
 
 
 def flat(tile):
@@ -43,9 +44,10 @@ def deal(copy, grouped, raw, first):
     )
 
 
-def deal_pair(copy, grouped, raw, first):
+def deal_pair(copy, grouped, raw, first, start):
+    count = raw.shape[2] // PACK
     copy(
-        out=grouped.rearrange("p t m j -> p m j t"),
+        out=grouped[:, :, start : start + count, :].rearrange("p t m j -> p m j t"),
         in_=raw.rearrange("p j (m t) -> p m j t", t=PACK)[:, :, :, first : first + 2],
     )
 
@@ -85,8 +87,11 @@ def tile_picked_fpn_none_lo_kernel(tc, xT, sT, w1, w2, offs, par, out_0, out_1, 
             raw = keep.tile([P, T], F32, name=f"x_raw{j}")
             nc.sync.dma_start(out=raw[:], in_=x_rows[:, j, :])
             x_raw.append(raw)
-        w1_raw = keep.tile([P, PACK, N], F32, name="w1_raw", tag="late", align_bytes=64)
-        nc.sync.dma_start(out=w1_raw[:], in_=w1.rearrange("(p j) c -> p j c", j=PACK))
+        w1_rows = w1.rearrange("(p j) c -> p j c", j=PACK)
+        w1_early = keep.tile([P, PACK, EARLY], F32, name="w1_early", tag="late", align_bytes=64)
+        nc.sync.dma_start(out=w1_early[:], in_=w1_rows[:, :, :EARLY])
+        w1_last = keep.tile([P, PACK, N - EARLY], F32, name="w1_last")
+        nc.sync.dma_start(out=w1_last[:], in_=w1_rows[:, :, EARLY:])
 
         w2_grouped = keep.tile([P, PACK, P, PACK], BF16, name="w2_grouped", align_bytes=64)
         deal(nc.vector.tensor_copy, w2_grouped, w2_raw[:], 0)
@@ -110,44 +115,52 @@ def tile_picked_fpn_none_lo_kernel(tc, xT, sT, w1, w2, offs, par, out_0, out_1, 
                 product(acc[:], w2_codes, w2_scales, t, s_codes[:, cols], s_scales[:, cols])
                 nc.scalar.copy(out=coarse[t][:, cols], in_=acc[:])
 
-        fetched = keep.tile([P, PACK, S], F32, name="fetched")
+        fetched_first = [keep.tile([P, HALF], F32, name=f"fetched{t}", tag=f"fetched{t}", align_bytes=64) for t in range(PACK)]
+        fetched_late = keep.tile([P, PACK, HALF], F32, name="fetched_late")
         for t in range(PACK):
-            for h in range(2):
+            for h, target in enumerate((fetched_first[t][:], fetched_late[:, t, :])):
                 entries = parents[:, h * (HALF // 16) : (h + 1) * (HALF // 16)]
-                nc.vector.tensor_copy(fetched[:, t, h * HALF : (h + 1) * HALF], coarse[t][:].indirect(entries))
+                nc.vector.tensor_copy(target, coarse[t][:].indirect(entries))
 
         halves = [slice(h * HALF, (h + 1) * HALF) for h in range(2)]
         entries = [picked[:, h * (HALF // 16) : (h + 1) * (HALF // 16)] for h in range(2)]
-        x_picked = keep.tile([P, PACK, S], BF16, name="x_picked")
+        x_picked = keep.tile([P, 3, S], BF16, name="x_picked")
         x_first = keep.tile([P, HALF, PACK], BF16, name="x_first", align_bytes=64)
         for j in (0, 1):
             nc.scalar.activation(x_picked[:, j, :], x_raw[j][:].indirect(picked[:]), COPY)
         weave(nc.scalar.copy, x_first[:, :, 0:2], x_picked[:, 0:2, halves[0]])
-        for j in (2, 3):
-            nc.vector.tensor_copy(x_first[:, :, j], x_raw[j][:].indirect(entries[0]))
-            nc.scalar.activation(x_picked[:, j, halves[1]], x_raw[j][:].indirect(entries[1]), COPY)
+        late = [slice(HALF + c * CHUNK, HALF + (c + 1) * CHUNK) for c in range(2)]
+        late_entries = [picked[:, cols.start // 16 : cols.stop // 16] for cols in late]
+        x_second = keep.tile([P, HALF, PACK], BF16, name="x_second", align_bytes=64)
+        nc.vector.tensor_copy(x_first[:, :, 2], x_raw[2][:].indirect(entries[0]))
+        nc.scalar.activation(x_picked[:, 2, halves[1]], x_raw[2][:].indirect(entries[1]), COPY)
+        weave(nc.scalar.copy, x_second[:, :, 0:3], x_picked[:, :, halves[1]])
+        nc.vector.tensor_copy(x_first[:, :, 3], x_raw[3][:].indirect(entries[0]))
+
+        def complete(c, tag):
+            last = keep.tile([P, CHUNK], BF16, name=f"x_last{c}", tag=tag, align_bytes=64)
+            nc.scalar.activation(last[:], x_raw[3][:].indirect(late_entries[c]), COPY)
+            nc.scalar.copy(out=x_second[:, c * CHUNK : (c + 1) * CHUNK, 3], in_=last[:])
+
+        complete(0, "third")
         x_codes = [keep.tile([P, HALF], U32, name="x_codes0", align_bytes=64)]
         x_scales = keep.tile([P, S], U8, name="x_scales", align_bytes=64)
         quantize(x_codes[0][:], x_scales[:, halves[0]], flat(x_first[:]))
 
-        late = [slice(HALF + c * CHUNK, HALF + (c + 1) * CHUNK) for c in range(2)]
-        x_third = keep.tile([P, CHUNK, PACK], BF16, name="x_third", align_bytes=64)
-        weave(nc.scalar.copy, x_third[:], x_picked[:, :, late[0]])
-
         w1_grouped = [keep.tile([P, 2, P, PACK], BF16, name=f"w1_grouped{u}", tag=f"dealt{u}", align_bytes=64) for u in range(2)]
-        deal_pair(nc.vector.tensor_copy, w1_grouped[0][:], w1_raw[:], 0)
-        deal_pair(nc.scalar.copy, w1_grouped[1][:], w1_raw[:], 2)
+        deal_pair(nc.scalar.copy, w1_grouped[0], w1_early[:], 0, 0)
+        deal_pair(nc.vector.tensor_copy, w1_grouped[0], w1_last[:], 0, EARLY // PACK)
+        deal_pair(nc.vector.tensor_copy, w1_grouped[1], w1_last[:], 2, EARLY // PACK)
+        deal_pair(nc.scalar.copy, w1_grouped[1], w1_early[:], 2, 0)
         w1_codes = keep.tile([P, N], U32, name="w1_codes", align_bytes=64)
         w1_scales = keep.tile([P, N], U8, name="w1_scales", align_bytes=64)
         for t in range(2):
             cols = slice(t * P, (t + 1) * P)
             quantize(w1_codes[:, cols], w1_scales[:, cols], flat(w1_grouped[0][:, t, :, :]))
-        x_codes.append(keep.tile([P, HALF], U32, name="x_codes1", tag="dealt0", align_bytes=64))
-        quantize(x_codes[1][:, :CHUNK], x_scales[:, late[0]], flat(x_third[:]))
+        x_codes.append(keep.tile([P, CHUNK], U32, name="x_codes1", tag="dealt0", align_bytes=64))
+        quantize(x_codes[1][:], x_scales[:, late[0]], flat(x_second[:, :CHUNK, :]))
         quantize(w1_codes[:, 2 * P :], w1_scales[:, 2 * P :], w1_grouped[1][:].rearrange("p t m j -> p (t m j)"))
-        x_fourth = keep.tile([P, CHUNK, PACK], BF16, name="x_fourth", tag="late", align_bytes=64)
-        weave(nc.scalar.copy, x_fourth[:], x_picked[:, :, late[1]])
-        quantize(x_codes[1][:, CHUNK:], x_scales[:, late[1]], flat(x_fourth[:]))
+        complete(1, "late")
 
         out_rows = out_0.rearrange("(p t) c -> p t c", t=PACK)
         out_words = out_1[0].rearrange("p c j -> p (c j)").bitcast(I32)
@@ -160,27 +173,30 @@ def tile_picked_fpn_none_lo_kernel(tc, xT, sT, w1, w2, offs, par, out_0, out_1, 
                 cols = slice(first, first + width)
                 acc = psum.tile([P, width], F32, name="acc")
                 product(acc[:], w1_codes, w1_scales, t, x_codes[0][:, cols], x_scales[:, cols])
-                nc.vector.tensor_tensor(results[0][:, t, cols], acc[:], fetched[:, t, cols], ADD)
+                nc.vector.tensor_tensor(results[0][:, t, cols], acc[:], fetched_first[t][:, cols], ADD)
             nc.sync.dma_start(out=out_rows[:, t, halves[0]], in_=results[0][:, t, :])
-        def wide(t):
-            acc = psum.tile([P, HALF], F32, name="acc")
-            product(acc[:], w1_codes, w1_scales, t, x_codes[1][:], x_scales[:, halves[1]])
-            nc.vector.tensor_tensor(results[1][:, t, :], acc[:], fetched[:, t, halves[1]], ADD)
-            nc.sync.dma_start(out=out_rows[:, t, halves[1]], in_=results[1][:, t, :])
+            if t == 1:
+                x_codes.append(keep.tile([P, CHUNK], U32, name="x_codes2", tag="fetched1", align_bytes=64))
+                quantize(x_codes[2][:], x_scales[:, late[1]], flat(x_second[:, CHUNK:, :]))
 
-        def paired(c):
+        def paired(c, first):
             part = slice(c * CHUNK, (c + 1) * CHUNK)
-            cols = slice(HALF + c * CHUNK, HALF + (c + 1) * CHUNK)
+            tiles = slice(first, first + 2)
             acc = psum.tile([P, 2, CHUNK], F32, name="acc")
             for u in range(2):
-                product(acc[:, u, :], w1_codes, w1_scales, 2 + u, x_codes[1][:, part], x_scales[:, cols])
-            nc.vector.tensor_tensor(results[1][:, 2:4, part], acc[:], fetched[:, 2:4, cols], ADD)
-            nc.sync.dma_start(out=out_rows[:, 2:4, cols], in_=results[1][:, 2:4, part])
+                product(acc[:, u, :], w1_codes, w1_scales, first + u, x_codes[1 + c][:], x_scales[:, late[c]])
+            nc.vector.tensor_tensor(results[1][:, tiles, part], acc[:], fetched_late[:, tiles, part], ADD)
 
-        paired(0)
-        wide(0)
-        wide(1)
-        paired(1)
+        paired(0, 2)
+        nc.sync.dma_start(out=out_rows[:, 2:4, late[0]], in_=results[1][:, 2:4, :CHUNK])
+        paired(0, 0)
+        for t in range(2):
+            acc = psum.tile([P, CHUNK], F32, name="acc")
+            product(acc[:], w1_codes, w1_scales, t, x_codes[2][:], x_scales[:, late[1]])
+            nc.vector.tensor_tensor(results[1][:, t, CHUNK:], acc[:], fetched_late[:, t, CHUNK:], ADD)
+            nc.sync.dma_start(out=out_rows[:, t, halves[1]], in_=results[1][:, t, :])
+        paired(1, 2)
+        nc.sync.dma_start(out=out_rows[:, 2:4, late[1]], in_=results[1][:, 2:4, CHUNK:])
         y_first = keep.tile([P, HALF, PACK], BF16, name="y_first", align_bytes=64)
         y_late = [keep.tile([P, CHUNK, PACK], BF16, name=f"y_late{c}", align_bytes=64) for c in range(2)]
         weave(nc.scalar.copy, y_first[:, :CHUNK, :], results[0][:, :, :CHUNK])

@@ -130,19 +130,25 @@ def tile_picked_fpn_none_lo_kernel(tc, xT, sT, w1, w2, offs, par, out_0, out_1, 
             nc.scalar.activation(x_picked[:, j, :], x_raw[j][:].indirect(picked[:]), COPY)
         weave(nc.scalar.copy, x_first[:, :, 0:2], x_picked[:, 0:2, halves[0]])
         late = [slice(HALF + c * CHUNK, HALF + (c + 1) * CHUNK) for c in range(2)]
-        late_entries = [picked[:, cols.start // 16 : cols.stop // 16] for cols in late]
         x_second = keep.tile([P, HALF, PACK], BF16, name="x_second", align_bytes=64)
         nc.vector.tensor_copy(x_first[:, :, 2], x_raw[2][:].indirect(entries[0]))
         nc.scalar.activation(x_picked[:, 2, halves[1]], x_raw[2][:].indirect(entries[1]), COPY)
         weave(nc.scalar.copy, x_second[:, :, 0:3], x_picked[:, :, halves[1]])
         nc.vector.tensor_copy(x_first[:, :, 3], x_raw[3][:].indirect(entries[0]))
 
-        def complete(c, tag):
-            last = keep.tile([P, CHUNK], BF16, name=f"x_last{c}", tag=tag, align_bytes=64)
-            nc.scalar.activation(last[:], x_raw[3][:].indirect(late_entries[c]), COPY)
-            nc.scalar.copy(out=x_second[:, c * CHUNK : (c + 1) * CHUNK, 3], in_=last[:])
+        def complete(c, tags):
+            width = CHUNK // len(tags)
+            steps = []
+            for u, tag in enumerate(tags):
+                first = c * CHUNK + u * width
+                last = keep.tile([P, width], BF16, name=f"x_last{c}{u}", tag=tag, align_bytes=64)
+                offsets = picked[:, (HALF + first) // 16 : (HALF + first + width) // 16]
+                nc.scalar.activation(last[:], x_raw[3][:].indirect(offsets), COPY)
+                steps.append((first, last))
+            for first, last in steps:
+                nc.scalar.copy(out=x_second[:, first : first + width, 3], in_=last[:])
 
-        complete(0, "third")
+        complete(0, ("dealt0", "dealt1"))
         x_codes = [keep.tile([P, HALF], U32, name="x_codes0", align_bytes=64)]
         x_scales = keep.tile([P, S], U8, name="x_scales", align_bytes=64)
         quantize(x_codes[0][:], x_scales[:, halves[0]], flat(x_first[:]))
@@ -160,7 +166,7 @@ def tile_picked_fpn_none_lo_kernel(tc, xT, sT, w1, w2, offs, par, out_0, out_1, 
         x_codes.append(keep.tile([P, CHUNK], U32, name="x_codes1", tag="dealt0", align_bytes=64))
         quantize(x_codes[1][:], x_scales[:, late[0]], flat(x_second[:, :CHUNK, :]))
         quantize(w1_codes[:, 2 * P :], w1_scales[:, 2 * P :], w1_grouped[1][:].rearrange("p t m j -> p (t m j)"))
-        complete(1, "late")
+        complete(1, ("late",))
 
         out_rows = out_0.rearrange("(p t) c -> p t c", t=PACK)
         out_words = out_1[0].rearrange("p c j -> p (c j)").bitcast(I32)

@@ -20,6 +20,8 @@ P = 128
 PACK = 4
 HALF = S // 2
 CHUNK = 256
+STEP = 128
+DEALT = 2 * P * PACK * 2
 SPARE = 16
 SHARE = 144
 EARLY = 352
@@ -56,6 +58,7 @@ def tile_picked_fpn_none_lo_kernel(tc, xT, sT, w1, w2, offs, par, out_0, out_1, 
     nc = tc.nc
     with ExitStack() as ctx:
         keep = ctx.enter_context(tc.tile_pool(name="keep", bufs=1))
+        shared = ctx.enter_context(tc.tile_pool(name="shared", bufs=1))
         psum = ctx.enter_context(tc.psum_pool(name="psum", bufs=8))
 
         def quantize(codes, scales, grouped):
@@ -136,24 +139,20 @@ def tile_picked_fpn_none_lo_kernel(tc, xT, sT, w1, w2, offs, par, out_0, out_1, 
         weave(nc.scalar.copy, x_second[:, :, 0:3], x_picked[:, :, halves[1]])
         nc.vector.tensor_copy(x_first[:, :, 3], x_raw[3][:].indirect(entries[0]))
 
-        def complete(c, tags):
-            width = CHUNK // len(tags)
-            steps = []
-            for u, tag in enumerate(tags):
-                first = c * CHUNK + u * width
-                last = keep.tile([P, width], BF16, name=f"x_last{c}{u}", tag=tag, align_bytes=64)
-                offsets = picked[:, (HALF + first) // 16 : (HALF + first + width) // 16]
-                nc.scalar.activation(last[:], x_raw[3][:].indirect(offsets), COPY)
-                steps.append((first, last))
-            for first, last in steps:
-                nc.scalar.copy(out=x_second[:, first : first + width, 3], in_=last[:])
-
-        complete(0, ("dealt0", "dealt1"))
-        x_codes = [keep.tile([P, HALF], U32, name="x_codes0", align_bytes=64)]
+        x_third = shared.tile([P, CHUNK], BF16, name="x_third", offset=DEALT - STEP, align_bytes=64)
+        for first in range(0, CHUNK, STEP):
+            offsets = picked[:, (HALF + first) // 16 : (HALF + first + STEP) // 16]
+            nc.scalar.activation(x_third[:, first : first + STEP], x_raw[3][:].indirect(offsets), COPY)
+        nc.gpsimd.tensor_scalar(x_second[:, :STEP, 3], x_third[:, :STEP], 1.0, 0.0, MULT, ADD)
+        nc.scalar.copy(out=x_second[:, STEP:CHUNK, 3], in_=x_third[:, STEP:])
+        x_codes = [shared.tile([P, HALF], U32, name="x_codes0", offset=DEALT, align_bytes=64)]
+        x_codes.append(keep.tile([P, CHUNK], U32, name="x_codes1", align_bytes=64))
         x_scales = keep.tile([P, S], U8, name="x_scales", align_bytes=64)
+        quantize(x_codes[1][:], x_scales[:, late[0]], flat(x_second[:, :CHUNK, :]))
         quantize(x_codes[0][:], x_scales[:, halves[0]], flat(x_first[:]))
 
-        w1_grouped = [keep.tile([P, 2, P, PACK], BF16, name=f"w1_grouped{u}", tag=f"dealt{u}", align_bytes=64) for u in range(2)]
+        w1_grouped = [shared.tile([P, 2, P, PACK], BF16, name="w1_grouped0", offset=0, align_bytes=64)]
+        w1_grouped.append(keep.tile([P, 2, P, PACK], BF16, name="w1_grouped1", align_bytes=64))
         deal_pair(nc.scalar.copy, w1_grouped[0], w1_early[:], 0, 0)
         deal_pair(nc.vector.tensor_copy, w1_grouped[0], w1_last[:], 0, EARLY // PACK)
         deal_pair(nc.vector.tensor_copy, w1_grouped[1], w1_last[:], 2, EARLY // PACK)
@@ -163,10 +162,13 @@ def tile_picked_fpn_none_lo_kernel(tc, xT, sT, w1, w2, offs, par, out_0, out_1, 
         for t in range(2):
             cols = slice(t * P, (t + 1) * P)
             quantize(w1_codes[:, cols], w1_scales[:, cols], flat(w1_grouped[0][:, t, :, :]))
-        x_codes.append(keep.tile([P, CHUNK], U32, name="x_codes1", tag="dealt0", align_bytes=64))
-        quantize(x_codes[1][:], x_scales[:, late[0]], flat(x_second[:, :CHUNK, :]))
         quantize(w1_codes[:, 2 * P :], w1_scales[:, 2 * P :], w1_grouped[1][:].rearrange("p t m j -> p (t m j)"))
-        complete(1, ("late",))
+        x_fourth = keep.tile([P, CHUNK], BF16, name="x_fourth", tag="late", align_bytes=64)
+        for first in range(0, CHUNK, STEP):
+            offsets = picked[:, (S - CHUNK + first) // 16 : (S - CHUNK + first + STEP) // 16]
+            nc.scalar.activation(x_fourth[:, first : first + STEP], x_raw[3][:].indirect(offsets), COPY)
+        for first in range(0, CHUNK, STEP):
+            nc.scalar.copy(out=x_second[:, CHUNK + first : CHUNK + first + STEP, 3], in_=x_fourth[:, first : first + STEP])
 
         out_rows = out_0.rearrange("(p t) c -> p t c", t=PACK)
         out_words = out_1[0].rearrange("p c j -> p (c j)").bitcast(I32)

@@ -149,6 +149,9 @@ def tile_picked_fpn_none_lo_kernel(tc, xT, sT, w1, w2, offs, par, out_0, out_1, 
         x_codes.append(keep.tile([P, CHUNK], U32, name="x_codes1", align_bytes=64))
         x_scales = keep.tile([P, S], U8, name="x_scales", align_bytes=64)
         quantize(x_codes[1][:], x_scales[:, late[0]], flat(x_second[:, :CHUNK, :]))
+        unread = psum.tile([P, 2, CHUNK], F32, name="acc")
+        for u in range(2):
+            product(unread[:, u, :], w2_codes, w2_scales, u, x_codes[1][:], x_scales[:, late[0]])
         quantize(x_codes[0][:], x_scales[:, halves[0]], flat(x_first[:]))
 
         w1_grouped = [shared.tile([P, 2, P, PACK], BF16, name="w1_grouped0", offset=0, align_bytes=64)]

@@ -222,5 +222,5 @@ def tile_picked_fpn_none_lo_kernel(tc, xT, sT, w1, w2, offs, par, out_0, out_1, 
             quantize(y_codes[:, cols], y_scales[:, cols], flat(y_late[c][:]))
         nc.sync.dma_start(out=out_words[:, halves[1]], in_=y_codes[:, halves[1]].bitcast(I32))
         scale_rows = out_2[0].bitcast(I32)
-        for q, queue in enumerate((nc.scalar, nc.scalar, nc.sync, nc.sync)):
+        for q, queue in enumerate((nc.scalar, nc.scalar, nc.scalar, nc.scalar)):
             queue.dma_start(out=scale_rows[4 * q : 4 * q + 4, :], in_=y_scales[32 * q : 32 * q + 4, :].bitcast(I32))

@@ -93,7 +93,7 @@ def tile_picked_fpn_none_lo_kernel(tc, xT, sT, w1, w2, offs, par, out_0, out_1, 
         w1_rows = w1.rearrange("(p j) c -> p j c", j=PACK)
         w1_early = keep.tile([P, PACK, EARLY], F32, name="w1_early", tag="late", align_bytes=64)
         nc.sync.dma_start(out=w1_early[:], in_=w1_rows[:, :, :EARLY])
-        w1_last = keep.tile([P, PACK, N - EARLY], F32, name="w1_last")
+        w1_last = keep.tile([P, PACK, N - EARLY], F32, name="w1_last", tag="last", align_bytes=64)
         nc.sync.dma_start(out=w1_last[:], in_=w1_rows[:, :, EARLY:])
 
         w2_grouped = keep.tile([P, PACK, P, PACK], BF16, name="w2_grouped", align_bytes=64)
@@ -126,33 +126,35 @@ def tile_picked_fpn_none_lo_kernel(tc, xT, sT, w1, w2, offs, par, out_0, out_1, 
                 nc.vector.tensor_copy(target, coarse[t][:].indirect(entries))
 
         halves = [slice(h * HALF, (h + 1) * HALF) for h in range(2)]
-        entries = [picked[:, h * (HALF // 16) : (h + 1) * (HALF // 16)] for h in range(2)]
+        late = [slice(HALF + c * CHUNK, HALF + (c + 1) * CHUNK) for c in range(2)]
+        middle = slice(CHUNK, CHUNK + HALF)
+        outer = (slice(0, CHUNK), late[1])
         x_picked = keep.tile([P, 3, S], BF16, name="x_picked")
-        x_first = keep.tile([P, HALF, PACK], BF16, name="x_first", align_bytes=64)
+        x_middle = keep.tile([P, HALF, PACK], BF16, name="x_middle", align_bytes=64)
+        x_outer = keep.tile([P, HALF, PACK], BF16, name="x_outer", align_bytes=64)
         for j in (0, 1):
             nc.scalar.activation(x_picked[:, j, :], x_raw[j][:].indirect(picked[:]), COPY)
-        weave(nc.scalar.copy, x_first[:, :, 0:2], x_picked[:, 0:2, halves[0]])
-        late = [slice(HALF + c * CHUNK, HALF + (c + 1) * CHUNK) for c in range(2)]
-        x_second = keep.tile([P, HALF, PACK], BF16, name="x_second", align_bytes=64)
-        nc.vector.tensor_copy(x_first[:, :, 2], x_raw[2][:].indirect(entries[0]))
-        nc.scalar.activation(x_picked[:, 2, halves[1]], x_raw[2][:].indirect(entries[1]), COPY)
-        weave(nc.scalar.copy, x_second[:, :, 0:3], x_picked[:, :, halves[1]])
-        nc.vector.tensor_copy(x_first[:, :, 3], x_raw[3][:].indirect(entries[0]))
+        weave(nc.scalar.copy, x_middle[:, :, 0:2], x_picked[:, 0:2, middle])
+        nc.vector.tensor_copy(x_middle[:, :, 2], x_raw[2][:].indirect(picked[:, middle.start // 16 : middle.stop // 16]))
+        for part in outer:
+            nc.scalar.activation(x_picked[:, 2, part], x_raw[2][:].indirect(picked[:, part.start // 16 : part.stop // 16]), COPY)
+        for c, part in enumerate(outer):
+            weave(nc.scalar.copy, x_outer[:, c * CHUNK : (c + 1) * CHUNK, 0:3], x_picked[:, :, part])
+        nc.vector.tensor_copy(x_middle[:, :, 3], x_raw[3][:].indirect(picked[:, middle.start // 16 : middle.stop // 16]))
 
-        x_third = shared.tile([P, CHUNK], BF16, name="x_third", offset=DEALT - STEP, align_bytes=64)
+        x_front = shared.tile([P, CHUNK], BF16, name="x_front", offset=DEALT - STEP, align_bytes=64)
         for first in range(0, CHUNK, STEP):
-            offsets = picked[:, (HALF + first) // 16 : (HALF + first + STEP) // 16]
-            nc.scalar.activation(x_third[:, first : first + STEP], x_raw[3][:].indirect(offsets), COPY)
-        nc.gpsimd.tensor_scalar(x_second[:, :STEP, 3], x_third[:, :STEP], 1.0, 0.0, MULT, ADD)
-        nc.scalar.copy(out=x_second[:, STEP:CHUNK, 3], in_=x_third[:, STEP:])
+            offsets = picked[:, first // 16 : (first + STEP) // 16]
+            nc.scalar.activation(x_front[:, first : first + STEP], x_raw[3][:].indirect(offsets), COPY)
+        nc.gpsimd.tensor_scalar(x_outer[:, :STEP, 3], x_front[:, :STEP], 1.0, 0.0, MULT, ADD)
+        nc.scalar.copy(out=x_outer[:, STEP:CHUNK, 3], in_=x_front[:, STEP:])
         x_codes = [shared.tile([P, HALF], U32, name="x_codes0", offset=DEALT, align_bytes=64)]
-        x_codes.append(keep.tile([P, CHUNK], U32, name="x_codes1", align_bytes=64))
         x_scales = keep.tile([P, S], U8, name="x_scales", align_bytes=64)
-        quantize(x_codes[1][:], x_scales[:, late[0]], flat(x_second[:, :CHUNK, :]))
+        quantize(x_codes[0][:, :CHUNK], x_scales[:, :CHUNK], flat(x_outer[:, :CHUNK, :]))
         unread = psum.tile([P, 2, CHUNK], F32, name="acc")
         for u in range(2):
-            product(unread[:, u, :], w2_codes, w2_scales, u, x_codes[1][:], x_scales[:, late[0]])
-        quantize(x_codes[0][:], x_scales[:, halves[0]], flat(x_first[:]))
+            product(unread[:, u, :], w2_codes, w2_scales, u, x_codes[0][:, :CHUNK], x_scales[:, :CHUNK])
+        quantize(x_codes[0][:, CHUNK:], x_scales[:, CHUNK:HALF], flat(x_middle[:, :CHUNK, :]))
 
         w1_grouped = [shared.tile([P, 2, P, PACK], BF16, name="w1_grouped0", offset=0, align_bytes=64)]
         w1_grouped.append(keep.tile([P, 2, P, PACK], BF16, name="w1_grouped1", align_bytes=64))
@@ -165,13 +167,15 @@ def tile_picked_fpn_none_lo_kernel(tc, xT, sT, w1, w2, offs, par, out_0, out_1, 
         for t in range(2):
             cols = slice(t * P, (t + 1) * P)
             quantize(w1_codes[:, cols], w1_scales[:, cols], flat(w1_grouped[0][:, t, :, :]))
+        x_codes.append(keep.tile([P, CHUNK], U32, name="x_codes1", tag="last", align_bytes=64))
+        quantize(x_codes[1][:], x_scales[:, late[0]], flat(x_middle[:, CHUNK:, :]))
         quantize(w1_codes[:, 2 * P :], w1_scales[:, 2 * P :], w1_grouped[1][:].rearrange("p t m j -> p (t m j)"))
         x_fourth = keep.tile([P, CHUNK], BF16, name="x_fourth", tag="late", align_bytes=64)
         for first in range(0, CHUNK, STEP):
             offsets = picked[:, (S - CHUNK + first) // 16 : (S - CHUNK + first + STEP) // 16]
             nc.scalar.activation(x_fourth[:, first : first + STEP], x_raw[3][:].indirect(offsets), COPY)
         for first in range(0, CHUNK, STEP):
-            nc.scalar.copy(out=x_second[:, CHUNK + first : CHUNK + first + STEP, 3], in_=x_fourth[:, first : first + STEP])
+            nc.scalar.copy(out=x_outer[:, CHUNK + first : CHUNK + first + STEP, 3], in_=x_fourth[:, first : first + STEP])
 
         out_rows = out_0.rearrange("(p t) c -> p t c", t=PACK)
         out_words = out_1[0].rearrange("p c j -> p (c j)").bitcast(I32)
@@ -188,7 +192,7 @@ def tile_picked_fpn_none_lo_kernel(tc, xT, sT, w1, w2, offs, par, out_0, out_1, 
             nc.sync.dma_start(out=out_rows[:, t, halves[0]], in_=results[0][:, t, :])
             if t == 1:
                 x_codes.append(keep.tile([P, CHUNK], U32, name="x_codes2", tag="fetched1", align_bytes=64))
-                quantize(x_codes[2][:], x_scales[:, late[1]], flat(x_second[:, CHUNK:, :]))
+                quantize(x_codes[2][:], x_scales[:, late[1]], flat(x_outer[:, CHUNK:, :]))
 
         def paired(c, first):
             part = slice(c * CHUNK, (c + 1) * CHUNK)

@@ -142,12 +142,14 @@ def tile_picked_fpn_none_lo_kernel(tc, xT, sT, w1, w2, offs, par, out_0, out_1, 
             weave(nc.scalar.copy, x_outer[:, c * CHUNK : (c + 1) * CHUNK, 0:3], x_picked[:, :, part])
         nc.vector.tensor_copy(x_middle[:, :, 3], x_raw[3][:].indirect(picked[:, middle.start // 16 : middle.stop // 16]))
 
-        x_front = shared.tile([P, CHUNK], BF16, name="x_front", offset=DEALT - STEP, align_bytes=64)
-        for first in range(0, CHUNK, STEP):
-            offsets = picked[:, first // 16 : (first + STEP) // 16]
-            nc.scalar.activation(x_front[:, first : first + STEP], x_raw[3][:].indirect(offsets), COPY)
-        nc.gpsimd.tensor_scalar(x_outer[:, :STEP, 3], x_front[:, :STEP], 1.0, 0.0, MULT, ADD)
-        nc.scalar.copy(out=x_outer[:, STEP:CHUNK, 3], in_=x_front[:, STEP:])
+        x_front = [
+            shared.tile([P, STEP], BF16, name=f"x_front{u}", offset=DEALT - STEP + 2 * STEP * u, align_bytes=64) for u in range(2)
+        ]
+        for u in range(2):
+            offsets = picked[:, u * STEP // 16 : (u + 1) * STEP // 16]
+            nc.scalar.activation(x_front[u][:], x_raw[3][:].indirect(offsets), COPY)
+        nc.scalar.copy(out=x_outer[:, :STEP, 3], in_=x_front[0][:])
+        nc.gpsimd.tensor_scalar(x_outer[:, STEP:CHUNK, 3], x_front[1][:], 1.0, 0.0, MULT, ADD)
         x_codes = [shared.tile([P, HALF], U32, name="x_codes0", offset=DEALT, align_bytes=64)]
         x_scales = keep.tile([P, S], U8, name="x_scales", align_bytes=64)
         quantize(x_codes[0][:, :CHUNK], x_scales[:, :CHUNK], flat(x_outer[:, :CHUNK, :]))

@@ -153,10 +153,9 @@ def tile_picked_fpn_none_lo_kernel(tc, xT, sT, w1, w2, offs, par, out_0, out_1, 
         x_codes = [shared.tile([P, HALF], U32, name="x_codes0", offset=DEALT, align_bytes=64)]
         x_scales = keep.tile([P, S], U8, name="x_scales", align_bytes=64)
         quantize(x_codes[0][:, :CHUNK], x_scales[:, :CHUNK], flat(x_outer[:, :CHUNK, :]))
-        unread = psum.tile([P, 2, CHUNK], F32, name="acc")
-        for u in range(2):
-            product(unread[:, u, :], w2_codes, w2_scales, u, x_codes[0][:, :CHUNK], x_scales[:, :CHUNK])
         quantize(x_codes[0][:, CHUNK:], x_scales[:, CHUNK:HALF], flat(x_middle[:, :CHUNK, :]))
+        unread = psum.tile([P, HALF], F32, name="acc")
+        product(unread[:], w2_codes, w2_scales, 0, x_codes[0][:], x_scales[:, halves[0]])
 
         w1_grouped = [shared.tile([P, 2, P, PACK], BF16, name="w1_grouped0", offset=0, align_bytes=64)]
         w1_grouped.append(keep.tile([P, 2, P, PACK], BF16, name="w1_grouped1", align_bytes=64))

from contextlib import ExitStack

import concourse.mybir as mybir

K, T, S, V, N = 512, 4096, 1024, 512, 512
FLOPS = 2 * K * N * (S + V)

F32 = mybir.dt.float32
BF16 = mybir.dt.bfloat16
I32 = mybir.dt.int32
U32 = mybir.dt.uint32
U16 = mybir.dt.uint16
U8 = mybir.dt.uint8
FP8X4 = mybir.dt.float8_e4m3fn_x4
COPY = mybir.ActivationFunctionType.Copy
ADD = mybir.AluOpType.add
MULT = mybir.AluOpType.mult

P = 128
PACK = 4
HALF = S // 2
CHUNK = 256
STEP = 128
DEALT = 2 * P * PACK * 2
SPARE = 16
SHARE = 144
EARLY = 352


def flat(tile):
    return tile.rearrange("p c j -> p (c j)")


def weave(copy, grouped, planes):
    copy(
        out=grouped.rearrange("p (c i) j -> p c j i", i=4),
        in_=planes.rearrange("p j (c i) -> p c j i", i=4),
    )


def deal(copy, grouped, raw, first):
    count = raw.shape[2] // PACK
    copy(
        out=grouped[:, :, first : first + count, :].rearrange("p t m j -> p m j t"),
        in_=raw.rearrange("p j (m t) -> p m j t", t=PACK),
    )


def deal_pair(copy, grouped, raw, first, start):
    count = raw.shape[2] // PACK
    copy(
        out=grouped[:, :, start : start + count, :].rearrange("p t m j -> p m j t"),
        in_=raw.rearrange("p j (m t) -> p m j t", t=PACK)[:, :, :, first : first + 2],
    )


def tile_picked_fpn_none_lo_kernel(tc, xT, sT, w1, w2, offs, par, out_0, out_1, out_2):
    nc = tc.nc
    with ExitStack() as ctx:
        keep = ctx.enter_context(tc.tile_pool(name="keep", bufs=1))
        shared = ctx.enter_context(tc.tile_pool(name="shared", bufs=1))
        psum = ctx.enter_context(tc.psum_pool(name="psum", bufs=8))

        def quantize(codes, scales, grouped):
            nc.vector.quantize_mx(out=codes.bitcast(FP8X4), scales=scales, in_=grouped)

        def product(acc, w_codes, w_scales, t, codes, scales):
            cols = slice(t * P, (t + 1) * P)
            nc.tensor.matmul_mx(
                out=acc,
                lhsT=w_codes[:, cols].bitcast(FP8X4),
                lhsT_scale=w_scales[:, cols],
                rhs=codes.bitcast(FP8X4),
                rhs_scale=scales,
                start=True,
                stop=True,
            )

        w2_raw = keep.tile([P, PACK, N], F32, name="w2_raw")
        nc.sync.dma_start(out=w2_raw[:], in_=w2.rearrange("(p j) c -> p j c", j=PACK))
        s_raw = keep.tile([P, PACK, V], F32, name="s_raw")
        nc.sync.dma_start(out=s_raw[:], in_=sT.rearrange("(p j) v -> p j v", j=PACK))
        parents = keep.tile([P, S // 16], U16, name="parents")
        nc.sync.dma_start(parents[:], par)
        picked = keep.tile([P, S // 16], U16, name="picked")
        nc.sync.dma_start(picked[:], offs)
        x_rows = xT.rearrange("(p j) c -> p j c", j=PACK)
        x_raw = []
        for j in range(PACK):
            raw = keep.tile([P, T], F32, name=f"x_raw{j}")
            nc.sync.dma_start(out=raw[:], in_=x_rows[:, j, :])
            x_raw.append(raw)
        w1_rows = w1.rearrange("(p j) c -> p j c", j=PACK)
        w1_early = keep.tile([P, PACK, EARLY], F32, name="w1_early", tag="late", align_bytes=64)
        nc.sync.dma_start(out=w1_early[:], in_=w1_rows[:, :, :EARLY])
        w1_last = keep.tile([P, PACK, N - EARLY], F32, name="w1_last", tag="last", align_bytes=64)
        nc.sync.dma_start(out=w1_last[:], in_=w1_rows[:, :, EARLY:])

        w2_grouped = keep.tile([P, PACK, P, PACK], BF16, name="w2_grouped", align_bytes=64)
        deal(nc.vector.tensor_copy, w2_grouped, w2_raw[:], 0)
        w2_codes = keep.tile([P, N], U32, name="w2_codes", align_bytes=64)
        w2_scales = keep.tile([P, N], U8, name="w2_scales", align_bytes=64)
        quantize(w2_codes[:], w2_scales[:], w2_grouped[:].rearrange("p t m j -> p (t m j)"))
        s_codes = keep.tile([P, V], U32, name="s_codes", align_bytes=64)
        s_scales = keep.tile([P, V], U8, name="s_scales", align_bytes=64)
        coarse = [keep.tile([P, V + SPARE], F32, name=f"coarse{t}") for t in range(PACK)]
        for t in range(PACK):
            nc.gpsimd.memset(coarse[t][:, V:], 0.0)
        for h, copy in enumerate((nc.vector.tensor_copy, nc.scalar.copy)):
            grouped = keep.tile([P, V // 2, PACK], BF16, name=f"s_grouped{h}", align_bytes=64)
            cols = slice(h * (V // 2), (h + 1) * (V // 2))
            weave(copy, grouped[:], s_raw[:, :, cols])
            quantize(s_codes[:, cols], s_scales[:, cols], flat(grouped[:]))
        for t in range(PACK):
            for h in range(2):
                cols = slice(h * (V // 2), (h + 1) * (V // 2))
                acc = psum.tile([P, V // 2], F32, name="acc")
                product(acc[:], w2_codes, w2_scales, t, s_codes[:, cols], s_scales[:, cols])
                nc.scalar.copy(out=coarse[t][:, cols], in_=acc[:])

        fetched_first = [keep.tile([P, HALF], F32, name=f"fetched{t}", tag=f"fetched{t}", align_bytes=64) for t in range(PACK)]
        fetched_late = keep.tile([P, PACK, HALF], F32, name="fetched_late")
        for t in range(PACK):
            for h, target in enumerate((fetched_first[t][:], fetched_late[:, t, :])):
                entries = parents[:, h * (HALF // 16) : (h + 1) * (HALF // 16)]
                nc.vector.tensor_copy(target, coarse[t][:].indirect(entries))

        halves = [slice(h * HALF, (h + 1) * HALF) for h in range(2)]
        late = [slice(HALF + c * CHUNK, HALF + (c + 1) * CHUNK) for c in range(2)]
        middle = slice(CHUNK, CHUNK + HALF)
        outer = (slice(0, CHUNK), late[1])
        x_picked = keep.tile([P, 3, S], BF16, name="x_picked")
        x_middle = keep.tile([P, HALF, PACK], BF16, name="x_middle", align_bytes=64)
        x_outer = keep.tile([P, HALF, PACK], BF16, name="x_outer", align_bytes=64)
        for j in (0, 1):
            nc.scalar.activation(x_picked[:, j, :], x_raw[j][:].indirect(picked[:]), COPY)
        weave(nc.scalar.copy, x_middle[:, :, 0:2], x_picked[:, 0:2, middle])
        nc.vector.tensor_copy(x_middle[:, :, 2], x_raw[2][:].indirect(picked[:, middle.start // 16 : middle.stop // 16]))
        for part in outer:
            nc.scalar.activation(x_picked[:, 2, part], x_raw[2][:].indirect(picked[:, part.start // 16 : part.stop // 16]), COPY)
        for c, part in enumerate(outer):
            weave(nc.scalar.copy, x_outer[:, c * CHUNK : (c + 1) * CHUNK, 0:3], x_picked[:, :, part])
        nc.vector.tensor_copy(x_middle[:, :, 3], x_raw[3][:].indirect(picked[:, middle.start // 16 : middle.stop // 16]))

        x_front = [
            shared.tile([P, STEP], BF16, name=f"x_front{u}", offset=DEALT - STEP + 2 * STEP * u, align_bytes=64) for u in range(2)
        ]
        for u in range(2):
            offsets = picked[:, u * STEP // 16 : (u + 1) * STEP // 16]
            nc.scalar.activation(x_front[u][:], x_raw[3][:].indirect(offsets), COPY)
        nc.scalar.copy(out=x_outer[:, :STEP, 3], in_=x_front[0][:])
        nc.gpsimd.tensor_scalar(x_outer[:, STEP:CHUNK, 3], x_front[1][:], 1.0, 0.0, MULT, ADD)
        x_codes = [shared.tile([P, HALF], U32, name="x_codes0", offset=DEALT, align_bytes=64)]
        x_scales = keep.tile([P, S], U8, name="x_scales", align_bytes=64)
        quantize(x_codes[0][:, :CHUNK], x_scales[:, :CHUNK], flat(x_outer[:, :CHUNK, :]))
        quantize(x_codes[0][:, CHUNK:], x_scales[:, CHUNK:HALF], flat(x_middle[:, :CHUNK, :]))
        unread = psum.tile([P, HALF], F32, name="acc")
        product(unread[:], w2_codes, w2_scales, 0, x_codes[0][:], x_scales[:, halves[0]])

        w1_grouped = [shared.tile([P, 2, P, PACK], BF16, name="w1_grouped0", offset=0, align_bytes=64)]
        w1_grouped.append(keep.tile([P, 2, P, PACK], BF16, name="w1_grouped1", align_bytes=64))
        deal_pair(nc.scalar.copy, w1_grouped[0], w1_early[:], 0, 0)
        deal_pair(nc.vector.tensor_copy, w1_grouped[0], w1_last[:], 0, EARLY // PACK)
        deal_pair(nc.vector.tensor_copy, w1_grouped[1], w1_last[:], 2, EARLY // PACK)
        deal_pair(nc.scalar.copy, w1_grouped[1], w1_early[:], 2, 0)
        w1_codes = keep.tile([P, N], U32, name="w1_codes", align_bytes=64)
        w1_scales = keep.tile([P, N], U8, name="w1_scales", align_bytes=64)
        for t in range(2):
            cols = slice(t * P, (t + 1) * P)
            quantize(w1_codes[:, cols], w1_scales[:, cols], flat(w1_grouped[0][:, t, :, :]))
        x_codes.append(keep.tile([P, CHUNK], U32, name="x_codes1", tag="last", align_bytes=64))
        quantize(x_codes[1][:], x_scales[:, late[0]], flat(x_middle[:, CHUNK:, :]))
        quantize(w1_codes[:, 2 * P :], w1_scales[:, 2 * P :], w1_grouped[1][:].rearrange("p t m j -> p (t m j)"))
        x_fourth = keep.tile([P, CHUNK], BF16, name="x_fourth", tag="late", align_bytes=64)
        for first in range(0, CHUNK, STEP):
            offsets = picked[:, (S - CHUNK + first) // 16 : (S - CHUNK + first + STEP) // 16]
            nc.scalar.activation(x_fourth[:, first : first + STEP], x_raw[3][:].indirect(offsets), COPY)
        for first in range(0, CHUNK, STEP):
            nc.scalar.copy(out=x_outer[:, CHUNK + first : CHUNK + first + STEP, 3], in_=x_fourth[:, first : first + STEP])

        out_rows = out_0.rearrange("(p t) c -> p t c", t=PACK)
        out_words = out_1[0].rearrange("p c j -> p (c j)").bitcast(I32)
        y_codes = keep.tile([P, S], U32, name="y_codes", align_bytes=64)
        y_scales = keep.tile([P, S], U8, name="y_scales", align_bytes=64)
        results = [keep.tile([P, PACK, HALF], F32, name=f"result{h}") for h in range(2)]
        for t in range(PACK):
            width = CHUNK if t == 0 else HALF
            for first in range(0, HALF, width):
                cols = slice(first, first + width)
                acc = psum.tile([P, width], F32, name="acc")
                product(acc[:], w1_codes, w1_scales, t, x_codes[0][:, cols], x_scales[:, cols])
                nc.vector.tensor_tensor(results[0][:, t, cols], acc[:], fetched_first[t][:, cols], ADD)
            nc.sync.dma_start(out=out_rows[:, t, halves[0]], in_=results[0][:, t, :])
            if t == 1:
                x_codes.append(keep.tile([P, CHUNK], U32, name="x_codes2", tag="fetched1", align_bytes=64))
                quantize(x_codes[2][:], x_scales[:, late[1]], flat(x_outer[:, CHUNK:, :]))

        def paired(c, first):
            part = slice(c * CHUNK, (c + 1) * CHUNK)
            tiles = slice(first, first + 2)
            acc = psum.tile([P, 2, CHUNK], F32, name="acc")
            for u in range(2):
                product(acc[:, u, :], w1_codes, w1_scales, first + u, x_codes[1 + c][:], x_scales[:, late[c]])
            nc.vector.tensor_tensor(results[1][:, tiles, part], acc[:], fetched_late[:, tiles, part], ADD)

        paired(0, 2)
        nc.sync.dma_start(out=out_rows[:, 2:4, late[0]], in_=results[1][:, 2:4, :CHUNK])
        paired(0, 0)
        for t in range(2):
            acc = psum.tile([P, CHUNK], F32, name="acc")
            product(acc[:], w1_codes, w1_scales, t, x_codes[2][:], x_scales[:, late[1]])
            nc.vector.tensor_tensor(results[1][:, t, CHUNK:], acc[:], fetched_late[:, t, CHUNK:], ADD)
            nc.sync.dma_start(out=out_rows[:, t, halves[1]], in_=results[1][:, t, :])
        paired(1, 2)
        nc.sync.dma_start(out=out_rows[:, 2:4, late[1]], in_=results[1][:, 2:4, CHUNK:])
        y_first = keep.tile([P, HALF, PACK], BF16, name="y_first", align_bytes=64)
        y_late = [keep.tile([P, CHUNK, PACK], BF16, name=f"y_late{c}", align_bytes=64) for c in range(2)]
        weave(nc.scalar.copy, y_first[:, :CHUNK, :], results[0][:, :, :CHUNK])
        nc.gpsimd.tensor_scalar(y_first[:, CHUNK:, :], results[0][:, :, CHUNK:].rearrange("p j c -> p c j"), 1.0, 0.0, MULT, ADD)
        weave(nc.scalar.copy, y_late[0][:], results[1][:, :, :CHUNK])
        weave(nc.scalar.copy, y_late[1][:, :SHARE, :], results[1][:, :, CHUNK : CHUNK + SHARE])
        weave(nc.vector.tensor_copy, y_late[1][:, SHARE:, :], results[1][:, :, CHUNK + SHARE :])
        quantize(y_codes[:, halves[0]], y_scales[:, halves[0]], flat(y_first[:]))
        nc.sync.dma_start(out=out_words[:, halves[0]], in_=y_codes[:, halves[0]].bitcast(I32))
        for c in range(2):
            cols = slice(HALF + c * CHUNK, HALF + (c + 1) * CHUNK)
            quantize(y_codes[:, cols], y_scales[:, cols], flat(y_late[c][:]))
        nc.sync.dma_start(out=out_words[:, halves[1]], in_=y_codes[:, halves[1]].bitcast(I32))
        scale_rows = out_2[0].bitcast(I32)
        for q, queue in enumerate((nc.scalar, nc.scalar, nc.scalar, nc.scalar)):
            queue.dma_start(out=scale_rows[4 * q : 4 * q + 4, :], in_=y_scales[32 * q : 32 * q + 4, :].bitcast(I32))
